import numpy as np
import ml_dtypes


def mxq(x, axis, fmt="e4m3"):
    dtype, down = {"e4m3": (ml_dtypes.float8_e4m3fn, 7), "e5m2": (ml_dtypes.float8_e5m2, 14)}[fmt]
    v = np.moveaxis(np.asarray(x, np.float32).astype(ml_dtypes.bfloat16).astype(np.float64), axis, -1)
    blocks = v.reshape(v.shape[:-1] + (-1, 32))
    amax = np.abs(blocks).max(-1, keepdims=True)
    byte = np.maximum(np.where(amax > 0, np.frexp(amax)[1] - 1 + 127, 0) - down, 1)
    scale = np.exp2(byte - 127.0)
    codes = (blocks / scale).astype(np.float32).astype(dtype).astype(np.float64)
    return np.moveaxis((codes * scale).reshape(v.shape), -1, axis)


WIDE = False


def mx_kscale(k):
    if not WIDE:
        return np.ones(k)
    levels = np.array([10, -10, 5, -5, 0])
    if k % 512:
        return np.exp2(np.random.permutation(np.resize(levels, k // 32))).repeat(32)
    a = np.empty((k // 512, 16))
    for p in range(k // 512):
        a[p, :8] = np.random.permutation(np.resize(levels, 8))
        for g in range(8):
            far = levels[np.abs(levels - a[p, g]) >= 10]
            a[p, g + 8] = far[np.random.randint(len(far))]
    return np.exp2(a.ravel()).repeat(32)


def f64(x):
    return np.asarray(x).astype(np.float64)


def striped(idx):
    return np.tile(idx.reshape(-1, 16).T, (8, 1)).astype(np.uint16)


def unstriped(offs):
    return offs[:16].T.reshape(-1).astype(np.int64)


def pack_weight(w):
    k, n = w.shape
    w = f64(np.asarray(w, np.float32).astype(ml_dtypes.bfloat16)).reshape(k // 32, 32, n)
    amax = np.abs(w).max(1)
    byte = np.clip(np.where(amax > 0, np.frexp(amax)[1] - 1 + 127 - 7, 1), 1, 254)
    scaled = (w * np.exp2(127.0 - byte)[:, None, :]).reshape(k, n).astype(np.float32)
    words = np.ascontiguousarray(scaled.reshape(k // 512, 128, 4, n).transpose(0, 1, 3, 2)).astype(ml_dtypes.float8_e4m3fn).view(np.uint8)
    return words, np.ascontiguousarray(byte.astype(np.uint8).reshape(k // 512, 16, n))


def unpack_weight(words, scales):
    g, p, n, _ = words.shape
    vals = np.ascontiguousarray(words).view(ml_dtypes.float8_e4m3fn).astype(np.float64) * np.repeat(np.exp2(scales.astype(np.float64) - 127.0), 8, axis=1)[..., None]
    return vals.transpose(0, 1, 3, 2).reshape(g * 512, n)


E2M1 = np.array([0.0, 0.5, 1.0, 1.5, 2.0, 3.0, 4.0, 6.0, -0.0, -0.5, -1.0, -1.5, -2.0, -3.0, -4.0, -6.0])


def pack_fp4(w):
    k, n = w.shape
    w = f64(np.asarray(w, np.float32).astype(ml_dtypes.bfloat16)).reshape(k // 32, 32, n)
    amax = np.abs(w).max(1)
    mant, ex = np.frexp(amax / 6.0)
    byte = np.clip(np.where(amax > 0, np.where(mant > 0.5, ex, ex - 1) + 127, 1), 1, 254)
    scaled = (w * np.exp2(127.0 - byte)[:, None, :]).reshape(k, n).astype(np.float32)
    c = np.ascontiguousarray(scaled.reshape(k // 512, 128, 4, n).transpose(0, 1, 3, 2)).astype(ml_dtypes.float4_e2m1fn).view(np.uint8) & 0xF
    words = (c[..., 0::2] | (c[..., 1::2] << 4)).reshape(k // 512, 128, 2 * n)
    return np.ascontiguousarray(words), np.ascontiguousarray(byte.astype(np.uint8).reshape(k // 512, 16, n))


def unpack_fp4(words, scales):
    g, _, n = scales.shape
    words = np.ascontiguousarray(words).reshape(g, 128, n, 2)
    nib = np.empty((g, 128, n, 4), np.uint8)
    nib[..., 0::2] = words & 0xF
    nib[..., 1::2] = words >> 4
    vals = E2M1[nib] * np.repeat(np.exp2(scales.astype(np.float64) - 127.0), 8, axis=1)[..., None]
    return vals.transpose(0, 1, 3, 2).reshape(g * 512, n)


def planes(y):
    n, m = y.shape
    v = y.astype(np.float32).astype(ml_dtypes.bfloat16).astype(np.float64).reshape(n // 32, 32, m)
    top = np.abs(v).max(1)
    byte = np.clip(np.where(top > 0, np.frexp(top)[1] - 1 + 127 - 7, 1), 1, 254)
    codes = (v * np.exp2(127.0 - byte)[:, None, :]).reshape(n, m).astype(np.float32).astype(ml_dtypes.float8_e4m3fn).view(np.uint8)
    words = codes.reshape(n // 512, 128, 4, m).transpose(0, 1, 3, 2)
    return np.ascontiguousarray(words), np.ascontiguousarray(byte.astype(np.uint8).reshape(n // 512, 16, m))


K, T, S, N, H, W = 512, 2048, 512, 512, 512, 384


def setup_inputs():
    n = np.random.standard_normal
    s = mx_kscale(K)[:, None]
    u = mx_kscale(S)
    packed_xT = pack_weight(n((K, T)) * s)
    packed_w1 = pack_fp4(n((S, N)) / np.sqrt(S) / u[:, None])
    return {
        "x_words": packed_xT[0],
        "x_scales": packed_xT[1],
        "wa": (n((K, H)) / np.sqrt(K) / s).astype(np.float32),
        "gt": (np.random.uniform(0.5, 1.5, (S, 1)) * u[:, None]).astype(np.float32),
        "w1_words": packed_w1[0],
        "w1_scales": packed_w1[1],
        "offs": striped(np.random.permutation(T)[:S]),
        "n1": striped(np.random.permutation(H)),
        "n2": striped(np.random.permutation(H)),
        "n3": striped(np.random.permutation(H)[:W]),
        "n4": striped(np.random.permutation(H)[:W]),
    }


def reference(x_words, x_scales, wa, gt, w1_words, w1_scales, offs, n1, n2, n3, n4):
    xq = unpack_weight(x_words, x_scales)[:, unstriped(offs)]
    y = xq.T @ mxq(f64(wa), 0, "e4m3")
    z = f64(gt) * (np.minimum(np.maximum(y, y[:, unstriped(n1)]), y[:, unstriped(n2)]))
    h = unpack_fp4(w1_words, w1_scales).T @ mxq(z, 0, "e4m3")
    old = h[:, unstriped(n3)]
    pa = h[:, unstriped(n4)]
    ra = old / (np.abs(pa) + 0.5)
    out = h.copy()
    out[:, unstriped(n3)] = ra
    return (out,) + planes(out)

@@ -1,0 +1,201 @@
+from contextlib import ExitStack
+
+import concourse.mybir as mybir
+
+K, T, S, N, H, W = 512, 2048, 512, 512, 512, 384
+FLOPS = 2 * K * S * H + 2 * S * N * H
+
+F32 = mybir.dt.float32
+BF16 = mybir.dt.bfloat16
+I32 = mybir.dt.int32
+U32 = mybir.dt.uint32
+U16 = mybir.dt.uint16
+U8 = mybir.dt.uint8
+FP8X4 = mybir.dt.float8_e4m3fn_x4
+FP4X4 = mybir.dt.float4_e2m1fn_x4
+ALU = mybir.AluOpType
+ACT = mybir.ActivationFunctionType
+
+P = 128
+PACK = 4
+WA_CHUNKS = ((0, 256), (256, 512))
+Z_CHUNKS = ((0, 256), (256, 384), (384, 512))
+
+
+def load_scale_rows(queue, plane, rows):
+    for q in range(4):
+        queue.dma_start(out=plane[32 * q : 32 * q + 4, :].bitcast(I32), in_=rows[4 * q : 4 * q + 4, :].bitcast(I32))
+
+
+def by_pairs(rows):
+    return rows.rearrange("p t (c i) -> p c t i", i=2)
+
+
+def woven_by_pairs(woven):
+    return woven.rearrange("p (c i) t -> p c t i", i=2)
+
+
+def tile_picked_tokminmxknorm_none_po_kernel(
+    tc, x_words, x_scales, wa, gt, w1_words, w1_scales, offs, n1, n2, n3, n4, out_0, out_1, out_2
+):
+    nc = tc.nc
+    with ExitStack() as ctx:
+        keep = ctx.enter_context(tc.tile_pool(name="keep", bufs=1))
+        psum = ctx.enter_context(tc.psum_pool(name="psum", bufs=1))
+
+        offs_sb = keep.tile([P, S // 16], U16)
+        nc.sync.dma_start(offs_sb[:], offs)
+        xs_table = keep.tile([P, T], U8)
+        nc.vector.memset(xs_table[:].bitcast(I32), 0)
+        load_scale_rows(nc.sync, xs_table, x_scales[0])
+        w1_raw = keep.tile([P, 2 * N], U8)
+        nc.sync.dma_start(out=w1_raw[:].bitcast(I32), in_=w1_words[0].bitcast(I32))
+        x_table = keep.tile([P, T], I32)
+        nc.scalar.dma_start(out=x_table[:], in_=x_words[0].rearrange("p n t -> p (n t)").bitcast(I32))
+        wa_rows = wa.rearrange("(p j) c -> p j c", j=PACK)
+        wa_raw = []
+        for lo, hi in WA_CHUNKS:
+            raw = keep.tile([P, PACK, hi - lo], F32, name="wa_raw%d" % lo)
+            nc.scalar.dma_start(out=raw[:], in_=wa_rows[:, :, lo:hi])
+            wa_raw.append(raw)
+
+        gate = keep.tile([P, PACK], F32)
+        nc.sync.dma_start(out=gate[:], in_=gt.rearrange("(p t) o -> p (t o)", t=PACK))
+        n1_sb = keep.tile([P, H // 16], U16)
+        nc.sync.dma_start(n1_sb[:], n1)
+        n2_sb = keep.tile([P, H // 16], U16)
+        nc.sync.dma_start(n2_sb[:], n2)
+        w1s_raw = keep.tile([P, N], U8)
+        nc.vector.memset(w1s_raw[:].bitcast(I32), 0)
+        load_scale_rows(nc.sync, w1s_raw, w1_scales[0])
+        n3_sb = keep.tile([P, W // 16], U16)
+        nc.sync.dma_start(n3_sb[:], n3)
+        n4_sb = keep.tile([P, W // 16], U16)
+        nc.sync.dma_start(n4_sb[:], n4)
+
+        xs_picked = keep.tile([P, S], U8)
+        nc.vector.tensor_copy(xs_picked[:], xs_table[:].indirect(offs_sb[:]))
+        w1_dealt = keep.tile([P, PACK, P, 2], U8, align_bytes=64)
+        nc.vector.tensor_copy(out=w1_dealt[:], in_=w1_raw[:].rearrange("p (m t b) -> p t m b", t=PACK, b=2))
+        xs_dealt = keep.tile([P, PACK, P], U8, align_bytes=64)
+        nc.vector.tensor_copy(out=xs_dealt[:], in_=xs_picked[:].rearrange("p (m t) -> p t m", t=PACK))
+        x_dealt = keep.tile([P, PACK, P], U32, align_bytes=64)
+        nc.vector.tensor_copy(x_dealt[:].rearrange("p t m -> p m t"), x_table[:].bitcast(U32).indirect(offs_sb[:]))
+        gate_abs = keep.tile([P, PACK], F32)
+        nc.vector.scalar_tensor_tensor(gate_abs[:], gate[:], -1.0, gate[:], ALU.mult, ALU.max)
+        gate_pos = keep.tile([P, PACK], F32)
+        nc.vector.tensor_scalar(gate_pos[:], gate[:], 0.0, 2.0, ALU.is_ge, ALU.mult)
+        w1s_dealt = keep.tile([P, PACK, P], U8, align_bytes=64)
+        nc.vector.tensor_copy(out=w1s_dealt[:], in_=w1s_raw[:].rearrange("p (m t) -> p t m", t=PACK))
+        widest = max(hi - lo for lo, hi in Z_CHUNKS)
+        signs = keep.tile([P, widest, PACK], BF16, align_bytes=64)
+        nc.vector.tensor_scalar(
+            signs[:], gate_pos[:].unsqueeze(1).to_broadcast([P, widest, PACK]), -1.0, None, ALU.add
+        )
+
+        y_banks = [psum.tile([P, H], F32, name="y_bank%d" % t, tag="bank%d" % t) for t in range(PACK)]
+        for (lo, hi), raw in zip(WA_CHUNKS, wa_raw):
+            width = hi - lo
+            woven = keep.tile([P, width, PACK], BF16, align_bytes=64, name="wa_woven%d" % lo)
+            split = width if lo == 0 else 96
+            nc.scalar.copy(out=woven_by_pairs(woven[:, :split, :]), in_=by_pairs(raw[:, :, :split]))
+            if split < width:
+                nc.vector.tensor_copy(out=woven_by_pairs(woven[:, split:, :]), in_=by_pairs(raw[:, :, split:]))
+            codes = keep.tile([P, width], U32, align_bytes=64, name="wa_codes%d" % lo)
+            scales = keep.tile([P, width], U8, align_bytes=64, name="wa_scales%d" % lo)
+            nc.vector.quantize_mx(
+                out=codes[:].bitcast(FP8X4), scales=scales[:], in_=woven[:].rearrange("p c t -> p (c t)")
+            )
+            for t in range(PACK):
+                nc.tensor.matmul_mx(
+                    out=y_banks[t][:, lo:hi],
+                    lhsT=x_dealt[:, t, :].bitcast(FP8X4),
+                    lhsT_scale=xs_dealt[:, t, :],
+                    rhs=codes[:].bitcast(FP8X4),
+                    rhs_scale=scales[:],
+                    start=True,
+                    stop=True,
+                )
+
+        y = keep.tile([P, PACK, H], F32)
+        for t in range(PACK):
+            if t % 2 == 0:
+                nc.scalar.activation(y[:, t, :], y_banks[t][:], ACT.Copy, scale=gate_abs[:, t : t + 1])
+            else:
+                nc.vector.tensor_scalar(y[:, t, :], y_banks[t][:], gate_abs[:, t : t + 1], None, ALU.mult)
+
+        h_banks = [psum.tile([P, H], F32, name="h_bank%d" % t, tag="bank%d" % (PACK + t)) for t in range(PACK)]
+        h_last = psum.tile([P, PACK, P], F32, name="h_last", tag="bank0")
+        h = [keep.tile([P, H], F32, name="h%d" % t) for t in range(PACK)]
+        last_lo = Z_CHUNKS[-1][0]
+        for lo, hi in Z_CHUNKS:
+            width = hi - lo
+            cols = slice(lo // 16, hi // 16)
+            y1 = keep.tile([P, PACK, width], F32, name="y1_%d" % lo)
+            y2 = keep.tile([P, PACK, width], F32, name="y2_%d" % lo)
+            for t in range(PACK):
+                nc.scalar.activation(y1[:, t, :], y[:, t, :].indirect(n1_sb[:, cols]), ACT.Copy)
+                if lo == 0:
+                    nc.vector.tensor_copy(y2[:, t, :], y[:, t, :].indirect(n2_sb[:, cols]))
+            if lo > 0:
+                for t in range(PACK):
+                    nc.scalar.activation(y2[:, t, :], y[:, t, :].indirect(n2_sb[:, cols]), ACT.Copy)
+            larger = keep.tile([P, PACK, width], F32, name="larger%d" % lo)
+            nc.vector.tensor_tensor(larger[:], y[:, :, lo:hi], y1[:], ALU.max)
+            z_abs = keep.tile([P, width, PACK], BF16, align_bytes=64, name="z_abs%d" % lo)
+            nc.vector.tensor_tensor(woven_by_pairs(z_abs[:]), by_pairs(larger[:]), by_pairs(y2[:]), ALU.min)
+            z = keep.tile([P, width, PACK], BF16, align_bytes=64, name="z%d" % lo)
+            nc.vector.tensor_tensor(z[:], z_abs[:], signs[:, :width, :], ALU.mult)
+            codes = keep.tile([P, width], U32, align_bytes=64, name="z_codes%d" % lo)
+            scales = keep.tile([P, width], U8, align_bytes=64, name="z_scales%d" % lo)
+            nc.vector.quantize_mx(
+                out=codes[:].bitcast(FP8X4), scales=scales[:], in_=z[:].rearrange("p c t -> p (c t)")
+            )
+            for t in range(PACK):
+                nc.tensor.matmul_mx(
+                    out=h_last[:, t, :] if lo == last_lo else h_banks[t][:, lo:hi],
+                    lhsT=w1_dealt[:, t, :, :].rearrange("p m b -> p (m b)").bitcast(FP4X4),
+                    lhsT_scale=w1s_dealt[:, t, :],
+                    rhs=codes[:].bitcast(FP8X4),
+                    rhs_scale=scales[:],
+                    start=True,
+                    stop=True,
+                )
+        for t in range(PACK):
+            nc.scalar.copy(out=h[t][:, :last_lo], in_=h_banks[t][:, :last_lo])
+        for t in range(PACK):
+            nc.vector.tensor_copy(out=h[t][:, last_lo:], in_=h_last[:, t, :])
+
+        out_rows = out_0.rearrange("(p t) c -> p t c", t=PACK)
+        out_woven = keep.tile([P, H, PACK], BF16, align_bytes=64)
+        ra = []
+        for t in range(PACK):
+            old = keep.tile([P, W], F32, name="old%d" % t)
+            nc.scalar.activation(old[:], h[t][:].indirect(n3_sb[:]), ACT.Copy)
+            pa = keep.tile([P, W], F32, name="pa%d" % t)
+            nc.vector.tensor_copy(pa[:], h[t][:].indirect(n4_sb[:]))
+            size = keep.tile([P, W], F32, name="size%d" % t)
+            nc.vector.scalar_tensor_tensor(size[:], pa[:], -1.0, pa[:], ALU.mult, ALU.max)
+            root = keep.tile([P, W], F32, name="root%d" % t)
+            nc.scalar.activation(root[:], size[:], ACT.Abs_reciprocal_sqrt, bias=0.5)
+            half_way = keep.tile([P, W], F32, name="half_way%d" % t)
+            nc.vector.tensor_tensor(half_way[:], old[:], root[:], ALU.mult)
+            done = keep.tile([P, W], F32, name="ra%d" % t)
+            nc.vector.tensor_tensor(done[:], half_way[:], root[:], ALU.mult)
+            ra.append(done)
+        for t in range(PACK):
+            nc.scalar.activation(h[t][:].indirect(n3_sb[:]), ra[t][:], ACT.Copy)
+            nc.sync.dma_start(out=out_rows[:, t, :], in_=h[t][:])
+            nc.vector.tensor_copy(out=out_woven[:, :, t], in_=h[t][:])
+
+        out_codes = keep.tile([P, H], U32, align_bytes=64)
+        out_scales = keep.tile([P, H], U8, align_bytes=64)
+        nc.vector.quantize_mx(
+            out=out_codes[:].bitcast(FP8X4), scales=out_scales[:], in_=out_woven[:].rearrange("p c t -> p (c t)")
+        )
+        nc.sync.dma_start(out=out_1[0].rearrange("p c t -> p (c t)").bitcast(I32), in_=out_codes[:].bitcast(I32))
+        for q in range(4):
+            queue = nc.scalar if q % 2 == 0 else nc.sync
+            queue.dma_start(
+                out=out_2[0][4 * q : 4 * q + 4, :].bitcast(I32), in_=out_scales[32 * q : 32 * q + 4, :].bitcast(I32)
+            )

@@ -19,7 +19,8 @@ ACT = mybir.ActivationFunctionType
 P = 128
 PACK = 4
 WA_CHUNKS = ((0, 256), (256, 512))
-Z_CHUNKS = ((0, 256), (256, 384), (384, 512))
+ZW = 128
+Z_CHUNKS = H // ZW
 
 
 def load_scale_rows(queue, plane, rows):
@@ -28,11 +29,11 @@ def load_scale_rows(queue, plane, rows):
 
 
 def by_pairs(rows):
-    return rows.rearrange("p t (c i) -> p c t i", i=2)
+    return rows.rearrange("p t (c i) -> p c t i", i=4)
 
 
 def woven_by_pairs(woven):
-    return woven.rearrange("p (c i) t -> p c t i", i=2)
+    return woven.rearrange("p (c i) t -> p c t i", i=4)
 
 
 def tile_picked_tokminmxknorm_none_po_kernel(
@@ -43,72 +44,67 @@ def tile_picked_tokminmxknorm_none_po_kernel(
         keep = ctx.enter_context(tc.tile_pool(name="keep", bufs=1))
         psum = ctx.enter_context(tc.psum_pool(name="psum", bufs=1))
 
-        offs_sb = keep.tile([P, S // 16], U16)
-        nc.sync.dma_start(offs_sb[:], offs)
         xs_table = keep.tile([P, T], U8)
         nc.vector.memset(xs_table[:].bitcast(I32), 0)
+        offs_sb = keep.tile([P, S // 16], U16)
+        nc.sync.dma_start(offs_sb[:], offs)
+        gate = keep.tile([P, PACK], F32)
+        nc.scalar.dma_start(out=gate[:], in_=gt.rearrange("(p t) o -> p (t o)", t=PACK))
         load_scale_rows(nc.sync, xs_table, x_scales[0])
         w1_raw = keep.tile([P, 2 * N], U8)
         nc.sync.dma_start(out=w1_raw[:].bitcast(I32), in_=w1_words[0].bitcast(I32))
         x_table = keep.tile([P, T], I32)
-        nc.scalar.dma_start(out=x_table[:], in_=x_words[0].rearrange("p n t -> p (n t)").bitcast(I32))
+        nc.sync.dma_start(out=x_table[:], in_=x_words[0].rearrange("p n t -> p (n t)").bitcast(I32))
         wa_rows = wa.rearrange("(p j) c -> p j c", j=PACK)
         wa_raw = []
         for lo, hi in WA_CHUNKS:
             raw = keep.tile([P, PACK, hi - lo], F32, name="wa_raw%d" % lo)
-            nc.scalar.dma_start(out=raw[:], in_=wa_rows[:, :, lo:hi])
+            nc.sync.dma_start(out=raw[:], in_=wa_rows[:, :, lo:hi])
             wa_raw.append(raw)
 
-        gate = keep.tile([P, PACK], F32)
-        nc.sync.dma_start(out=gate[:], in_=gt.rearrange("(p t) o -> p (t o)", t=PACK))
         n1_sb = keep.tile([P, H // 16], U16)
         nc.sync.dma_start(n1_sb[:], n1)
         n2_sb = keep.tile([P, H // 16], U16)
         nc.sync.dma_start(n2_sb[:], n2)
         w1s_raw = keep.tile([P, N], U8)
-        nc.vector.memset(w1s_raw[:].bitcast(I32), 0)
+        nc.gpsimd.memset(w1s_raw[:].bitcast(I32), 0)
         load_scale_rows(nc.sync, w1s_raw, w1_scales[0])
         n3_sb = keep.tile([P, W // 16], U16)
         nc.sync.dma_start(n3_sb[:], n3)
         n4_sb = keep.tile([P, W // 16], U16)
         nc.sync.dma_start(n4_sb[:], n4)
 
-        xs_picked = keep.tile([P, S], U8)
-        nc.vector.tensor_copy(xs_picked[:], xs_table[:].indirect(offs_sb[:]))
         w1_dealt = keep.tile([P, PACK, P, 2], U8, align_bytes=64)
         nc.vector.tensor_copy(out=w1_dealt[:], in_=w1_raw[:].rearrange("p (m t b) -> p t m b", t=PACK, b=2))
+        xs_picked = keep.tile([P, S], U8)
+        nc.vector.tensor_copy(xs_picked[:], xs_table[:].indirect(offs_sb[:]))
         xs_dealt = keep.tile([P, PACK, P], U8, align_bytes=64)
         nc.vector.tensor_copy(out=xs_dealt[:], in_=xs_picked[:].rearrange("p (m t) -> p t m", t=PACK))
         x_dealt = keep.tile([P, PACK, P], U32, align_bytes=64)
         nc.vector.tensor_copy(x_dealt[:].rearrange("p t m -> p m t"), x_table[:].bitcast(U32).indirect(offs_sb[:]))
-        gate_abs = keep.tile([P, PACK], F32)
-        nc.vector.scalar_tensor_tensor(gate_abs[:], gate[:], -1.0, gate[:], ALU.mult, ALU.max)
-        gate_pos = keep.tile([P, PACK], F32)
-        nc.vector.tensor_scalar(gate_pos[:], gate[:], 0.0, 2.0, ALU.is_ge, ALU.mult)
-        w1s_dealt = keep.tile([P, PACK, P], U8, align_bytes=64)
-        nc.vector.tensor_copy(out=w1s_dealt[:], in_=w1s_raw[:].rearrange("p (m t) -> p t m", t=PACK))
-        widest = max(hi - lo for lo, hi in Z_CHUNKS)
-        signs = keep.tile([P, widest, PACK], BF16, align_bytes=64)
-        nc.vector.tensor_scalar(
-            signs[:], gate_pos[:].unsqueeze(1).to_broadcast([P, widest, PACK]), -1.0, None, ALU.add
-        )
 
-        y_banks = [psum.tile([P, H], F32, name="y_bank%d" % t, tag="bank%d" % t) for t in range(PACK)]
-        for (lo, hi), raw in zip(WA_CHUNKS, wa_raw):
+        gate_abs = keep.tile([P, PACK], F32)
+        nc.scalar.activation(gate_abs[:], gate[:], ACT.Abs)
+        signs = keep.tile([P, PACK], BF16)
+        nc.scalar.activation(signs[:], gate[:], ACT.Sign)
+
+        y = keep.tile([P, PACK, H], F32)
+        y_banks = []
+        for half, ((lo, hi), raw) in enumerate(zip(WA_CHUNKS, wa_raw)):
             width = hi - lo
-            woven = keep.tile([P, width, PACK], BF16, align_bytes=64, name="wa_woven%d" % lo)
-            split = width if lo == 0 else 96
+            woven = keep.tile([P, width, PACK], BF16, align_bytes=64, name="wa_woven%d" % lo, tag="wa_woven%d" % lo)
+            split = 96
             nc.scalar.copy(out=woven_by_pairs(woven[:, :split, :]), in_=by_pairs(raw[:, :, :split]))
-            if split < width:
-                nc.vector.tensor_copy(out=woven_by_pairs(woven[:, split:, :]), in_=by_pairs(raw[:, :, split:]))
+            nc.vector.tensor_copy(out=woven_by_pairs(woven[:, split:, :]), in_=by_pairs(raw[:, :, split:]))
             codes = keep.tile([P, width], U32, align_bytes=64, name="wa_codes%d" % lo)
             scales = keep.tile([P, width], U8, align_bytes=64, name="wa_scales%d" % lo)
             nc.vector.quantize_mx(
                 out=codes[:].bitcast(FP8X4), scales=scales[:], in_=woven[:].rearrange("p c t -> p (c t)")
             )
             for t in range(PACK):
+                bank = psum.tile([P, width], F32, name="y_bank%d_%d" % (half, t), tag="bank%d" % (PACK * half + t))
                 nc.tensor.matmul_mx(
-                    out=y_banks[t][:, lo:hi],
+                    out=bank[:],
                     lhsT=x_dealt[:, t, :].bitcast(FP8X4),
                     lhsT_scale=xs_dealt[:, t, :],
                     rhs=codes[:].bitcast(FP8X4),
@@ -116,44 +112,50 @@ def tile_picked_tokminmxknorm_none_po_kernel(
                     start=True,
                     stop=True,
                 )
-
-        y = keep.tile([P, PACK, H], F32)
-        for t in range(PACK):
-            if t % 2 == 0:
-                nc.scalar.activation(y[:, t, :], y_banks[t][:], ACT.Copy, scale=gate_abs[:, t : t + 1])
+                y_banks.append((half, t, lo, hi, bank))
+        for half, t, lo, hi, bank in y_banks:
+            if half == 0 or t % 2 == 0:
+                nc.scalar.activation(y[:, t, lo:hi], bank[:], ACT.Copy, scale=gate_abs[:, t : t + 1])
             else:
-                nc.vector.tensor_scalar(y[:, t, :], y_banks[t][:], gate_abs[:, t : t + 1], None, ALU.mult)
+                nc.vector.tensor_scalar(y[:, t, lo:hi], bank[:], gate_abs[:, t : t + 1], None, ALU.mult)
+        w1s_dealt = keep.tile([P, PACK, P], U8, align_bytes=64, tag="wa_woven%d" % WA_CHUNKS[-1][0])
+        nc.vector.tensor_copy(out=w1s_dealt[:], in_=w1s_raw[:].rearrange("p (m t) -> p t m", t=PACK))
 
-        h_banks = [psum.tile([P, H], F32, name="h_bank%d" % t, tag="bank%d" % (PACK + t)) for t in range(PACK)]
-        h_last = psum.tile([P, PACK, P], F32, name="h_last", tag="bank0")
         h = [keep.tile([P, H], F32, name="h%d" % t) for t in range(PACK)]
-        last_lo = Z_CHUNKS[-1][0]
-        for lo, hi in Z_CHUNKS:
-            width = hi - lo
-            cols = slice(lo // 16, hi // 16)
-            y1 = keep.tile([P, PACK, width], F32, name="y1_%d" % lo)
-            y2 = keep.tile([P, PACK, width], F32, name="y2_%d" % lo)
-            for t in range(PACK):
-                nc.scalar.activation(y1[:, t, :], y[:, t, :].indirect(n1_sb[:, cols]), ACT.Copy)
-                if lo == 0:
-                    nc.vector.tensor_copy(y2[:, t, :], y[:, t, :].indirect(n2_sb[:, cols]))
-            if lo > 0:
-                for t in range(PACK):
-                    nc.scalar.activation(y2[:, t, :], y[:, t, :].indirect(n2_sb[:, cols]), ACT.Copy)
-            larger = keep.tile([P, PACK, width], F32, name="larger%d" % lo)
-            nc.vector.tensor_tensor(larger[:], y[:, :, lo:hi], y1[:], ALU.max)
-            z_abs = keep.tile([P, width, PACK], BF16, align_bytes=64, name="z_abs%d" % lo)
-            nc.vector.tensor_tensor(woven_by_pairs(z_abs[:]), by_pairs(larger[:]), by_pairs(y2[:]), ALU.min)
-            z = keep.tile([P, width, PACK], BF16, align_bytes=64, name="z%d" % lo)
-            nc.vector.tensor_tensor(z[:], z_abs[:], signs[:, :width, :], ALU.mult)
-            codes = keep.tile([P, width], U32, align_bytes=64, name="z_codes%d" % lo)
-            scales = keep.tile([P, width], U8, align_bytes=64, name="z_scales%d" % lo)
+        h_early = [psum.tile([P, 2, ZW], F32, name="h_early%d" % t, tag="bank%d" % t) for t in range(PACK)]
+        h_late = [psum.tile([P, 2, ZW], F32, name="h_late%d" % t, tag="bank%d" % (PACK + t)) for t in range(PACK)]
+        y1 = [keep.tile([P, PACK, ZW], F32, name="y1_%d" % c) for c in range(Z_CHUNKS)]
+        y2 = [keep.tile([P, PACK, ZW], F32, name="y2_%d" % c) for c in range(Z_CHUNKS)]
+        larger = [keep.tile([P, PACK, ZW], F32, name="larger%d" % c) for c in range(Z_CHUNKS)]
+        z_abs = [keep.tile([P, ZW, PACK], BF16, align_bytes=64, name="z_abs%d" % c) for c in range(Z_CHUNKS)]
+        z = [keep.tile([P, ZW, PACK], BF16, align_bytes=64, name="z%d" % c) for c in range(Z_CHUNKS)]
+
+        def fetch(on_scalar, dst, offsets, c, rows):
+            for t in rows:
+                window = y[:, t, :].indirect(offsets[:, c * ZW // 16 : (c + 1) * ZW // 16])
+                if on_scalar:
+                    nc.scalar.activation(dst[c][:, t, :], window, ACT.Copy)
+                else:
+                    nc.vector.tensor_copy(dst[c][:, t, :], window)
+
+        def take_max(c):
+            nc.vector.tensor_tensor(larger[c][:], y[:, :, c * ZW : (c + 1) * ZW], y1[c][:], ALU.max)
+
+        def take_min(c):
+            nc.vector.tensor_tensor(woven_by_pairs(z_abs[c][:]), by_pairs(larger[c][:]), by_pairs(y2[c][:]), ALU.min)
+
+        def give_sign(c):
+            nc.vector.tensor_tensor(z[c][:], z_abs[c][:], signs[:].unsqueeze(1).to_broadcast([P, ZW, PACK]), ALU.mult)
+
+        def multiply(c):
+            codes = keep.tile([P, ZW], U32, align_bytes=64, name="z_codes%d" % c)
+            scales = keep.tile([P, ZW], U8, align_bytes=64, name="z_scales%d" % c)
             nc.vector.quantize_mx(
-                out=codes[:].bitcast(FP8X4), scales=scales[:], in_=z[:].rearrange("p c t -> p (c t)")
+                out=codes[:].bitcast(FP8X4), scales=scales[:], in_=z[c][:].rearrange("p c t -> p (c t)")
             )
             for t in range(PACK):
                 nc.tensor.matmul_mx(
-                    out=h_last[:, t, :] if lo == last_lo else h_banks[t][:, lo:hi],
+                    out=h_early[t][:, c, :] if c < 2 else h_late[t][:, c - 2, :],
                     lhsT=w1_dealt[:, t, :, :].rearrange("p m b -> p (m b)").bitcast(FP4X4),
                     lhsT_scale=w1s_dealt[:, t, :],
                     rhs=codes[:].bitcast(FP8X4),
@@ -161,31 +163,87 @@ def tile_picked_tokminmxknorm_none_po_kernel(
                     start=True,
                     stop=True,
                 )
+
+        every_row = range(PACK)
+        for c in range(Z_CHUNKS):
+            fetch(True, y1, n1_sb, c, every_row)
+        fetch(True, y2, n2_sb, Z_CHUNKS - 1, every_row)
+        fetch(False, y2, n2_sb, 0, every_row)
+        fetch(False, y2, n2_sb, 1, every_row)
+        take_max(0)
+        fetch(False, y2, n2_sb, 2, range(0, 2))
+        take_min(0)
+        fetch(False, y2, n2_sb, 2, range(2, 4))
+        for c in range(Z_CHUNKS):
+            give_sign(c)
+            if c + 1 < Z_CHUNKS:
+                if c == 0:
+                    take_max(c + 1)
+                multiply(c)
+                take_min(c + 1)
+                if c + 2 < Z_CHUNKS:
+                    take_max(c + 2)
+            else:
+                multiply(c)
         for t in range(PACK):
-            nc.scalar.copy(out=h[t][:, :last_lo], in_=h_banks[t][:, :last_lo])
-        for t in range(PACK):
-            nc.vector.tensor_copy(out=h[t][:, last_lo:], in_=h_last[:, t, :])
+            nc.scalar.copy(out=h[t][:, : 2 * ZW], in_=h_early[t][:].rearrange("p c w -> p (c w)"))
+        nc.scalar.copy(out=h[0][:, 2 * ZW :], in_=h_late[0][:].rearrange("p c w -> p (c w)"))
 
         out_rows = out_0.rearrange("(p t) c -> p t c", t=PACK)
-        out_woven = keep.tile([P, H, PACK], BF16, align_bytes=64)
-        ra = []
-        for t in range(PACK):
-            old = keep.tile([P, W], F32, name="old%d" % t)
-            nc.scalar.activation(old[:], h[t][:].indirect(n3_sb[:]), ACT.Copy)
-            pa = keep.tile([P, W], F32, name="pa%d" % t)
-            nc.vector.tensor_copy(pa[:], h[t][:].indirect(n4_sb[:]))
-            size = keep.tile([P, W], F32, name="size%d" % t)
-            nc.vector.scalar_tensor_tensor(size[:], pa[:], -1.0, pa[:], ALU.mult, ALU.max)
-            root = keep.tile([P, W], F32, name="root%d" % t)
-            nc.scalar.activation(root[:], size[:], ACT.Abs_reciprocal_sqrt, bias=0.5)
-            half_way = keep.tile([P, W], F32, name="half_way%d" % t)
-            nc.vector.tensor_tensor(half_way[:], old[:], root[:], ALU.mult)
-            done = keep.tile([P, W], F32, name="ra%d" % t)
-            nc.vector.tensor_tensor(done[:], half_way[:], root[:], ALU.mult)
-            ra.append(done)
-        for t in range(PACK):
+        size = [keep.tile([P, W], F32, name="size%d" % t) for t in range(PACK)]
+        old = [keep.tile([P, W], F32, name="old%d" % t) for t in range(2)] + size[:2]
+        ra = [keep.tile([P, W], F32, name="ra%d" % t) for t in range(PACK)]
+        root = [keep.tile([P, W], F32, name="root%d" % u) for u in range(2)]
+        work = [keep.tile([P, W], F32, align_bytes=64, name="work%d" % u, tag="work%d" % u) for u in range(2)]
+
+        def last_columns(t):
+            nc.vector.tensor_copy(out=h[t][:, 2 * ZW :], in_=h_late[t][:].rearrange("p c w -> p (c w)"))
+
+        def fetch_old(t):
+            nc.scalar.activation(old[t][:], h[t][:].indirect(n3_sb[:]), ACT.Copy)
+
+        def fetch_pa(t):
+            nc.vector.tensor_copy(work[t % 2][:], h[t][:].indirect(n4_sb[:]))
+
+        def take_size(t):
+            nc.vector.scalar_tensor_tensor(size[t][:], work[t % 2][:], -1.0, work[t % 2][:], ALU.mult, ALU.max)
+
+        def take_root(t):
+            nc.scalar.activation(root[t % 2][:], size[t][:], ACT.Abs_reciprocal_sqrt, bias=0.5)
+
+        def first_factor(t):
+            nc.vector.tensor_tensor(work[t % 2][:], old[t][:], root[t % 2][:], ALU.mult)
+
+        def second_factor(t):
+            nc.vector.tensor_tensor(ra[t][:], work[t % 2][:], root[t % 2][:], ALU.mult)
+
+        def put_back(t):
             nc.scalar.activation(h[t][:].indirect(n3_sb[:]), ra[t][:], ACT.Copy)
             nc.sync.dma_start(out=out_rows[:, t, :], in_=h[t][:])
+
+        last_columns(1)
+        fetch_old(0)
+        fetch_pa(0)
+        take_size(0)
+        fetch_old(1)
+        take_root(0)
+        last_columns(2)
+        last_columns(3)
+        fetch_pa(1)
+        fetch_old(2)
+        for t in range(PACK):
+            first_factor(t)
+            if t + 1 < PACK:
+                take_size(t + 1)
+                take_root(t + 1)
+            if t == 0:
+                fetch_old(3)
+            second_factor(t)
+            put_back(t)
+            if t + 2 < PACK:
+                fetch_pa(t + 2)
+        out_woven = keep.tile([P, H, PACK], BF16, align_bytes=64, tag="work1")
+        for t in range(PACK):
             nc.vector.tensor_copy(out=out_woven[:, :, t], in_=h[t][:])
 
         out_codes = keep.tile([P, H], U32, align_bytes=64)

@@ -83,6 +83,8 @@ def tile_picked_tokminmxknorm_none_po_kernel(
         x_dealt = keep.tile([P, PACK, P], U32, align_bytes=64)
         nc.vector.tensor_copy(x_dealt[:].rearrange("p t m -> p m t"), x_table[:].bitcast(U32).indirect(offs_sb[:]))
 
+        warm = keep.tile([P, 1], F32)
+        nc.scalar.activation(warm[:], gate[:, 0:1], ACT.Abs_reciprocal_sqrt, bias=0.5)
         gate_abs = keep.tile([P, PACK], F32)
         nc.scalar.activation(gate_abs[:], gate[:], ACT.Abs)
         signs = keep.tile([P, PACK], BF16)
@@ -125,7 +127,9 @@ def tile_picked_tokminmxknorm_none_po_kernel(
         h_early = [psum.tile([P, 2, ZW], F32, name="h_early%d" % t, tag="bank%d" % t) for t in range(PACK)]
         h_late = [psum.tile([P, 2, ZW], F32, name="h_late%d" % t, tag="bank%d" % (PACK + t)) for t in range(PACK)]
         y1 = [keep.tile([P, PACK, ZW], F32, name="y1_%d" % c) for c in range(Z_CHUNKS)]
-        y2 = [keep.tile([P, PACK, ZW], F32, name="y2_%d" % c) for c in range(Z_CHUNKS)]
+        y2_early = keep.tile([P, PACK, 2 * ZW], F32)
+        y2 = [y2_early[:, :, :ZW], y2_early[:, :, ZW:]]
+        y2.extend(keep.tile([P, PACK, ZW], F32, name="y2_%d" % c)[:] for c in range(2, Z_CHUNKS))
         larger = [keep.tile([P, PACK, ZW], F32, name="larger%d" % c) for c in range(Z_CHUNKS)]
         z_abs = [keep.tile([P, ZW, PACK], BF16, align_bytes=64, name="z_abs%d" % c) for c in range(Z_CHUNKS)]
         z = [keep.tile([P, ZW, PACK], BF16, align_bytes=64, name="z%d" % c) for c in range(Z_CHUNKS)]
@@ -142,7 +146,7 @@ def tile_picked_tokminmxknorm_none_po_kernel(
             nc.vector.tensor_tensor(larger[c][:], y[:, :, c * ZW : (c + 1) * ZW], y1[c][:], ALU.max)
 
         def take_min(c):
-            nc.vector.tensor_tensor(woven_by_pairs(z_abs[c][:]), by_pairs(larger[c][:]), by_pairs(y2[c][:]), ALU.min)
+            nc.vector.tensor_tensor(woven_by_pairs(z_abs[c][:]), by_pairs(larger[c][:]), by_pairs(y2[c]), ALU.min)
 
         def give_sign(c):
             nc.vector.tensor_tensor(z[c][:], z_abs[c][:], signs[:].unsqueeze(1).to_broadcast([P, ZW, PACK]), ALU.mult)
@@ -165,33 +169,32 @@ def tile_picked_tokminmxknorm_none_po_kernel(
                 )
 
         every_row = range(PACK)
-        for c in range(Z_CHUNKS):
+        for c in range(3):
             fetch(True, y1, n1_sb, c, every_row)
-        fetch(True, y2, n2_sb, Z_CHUNKS - 1, every_row)
-        fetch(False, y2, n2_sb, 0, every_row)
-        fetch(False, y2, n2_sb, 1, every_row)
+        fetch(True, y2, n2_sb, 2, range(2, 4))
+        fetch(True, y1, n1_sb, 3, every_row)
+        fetch(True, y2, n2_sb, 3, every_row)
+        for t in every_row:
+            nc.vector.tensor_copy(y2_early[:, t, :], y[:, t, :].indirect(n2_sb[:, : 2 * ZW // 16]))
         take_max(0)
-        fetch(False, y2, n2_sb, 2, range(0, 2))
+        fetch(False, y2, n2_sb, 2, range(0, 1))
         take_min(0)
-        fetch(False, y2, n2_sb, 2, range(2, 4))
+        fetch(False, y2, n2_sb, 2, range(1, 2))
+        take_max(1)
         for c in range(Z_CHUNKS):
             give_sign(c)
             if c + 1 < Z_CHUNKS:
-                if c == 0:
-                    take_max(c + 1)
-                multiply(c)
                 take_min(c + 1)
-                if c + 2 < Z_CHUNKS:
-                    take_max(c + 2)
-            else:
-                multiply(c)
+            multiply(c)
+            if c + 2 < Z_CHUNKS:
+                take_max(c + 2)
         for t in range(PACK):
             nc.scalar.copy(out=h[t][:, : 2 * ZW], in_=h_early[t][:].rearrange("p c w -> p (c w)"))
         nc.scalar.copy(out=h[0][:, 2 * ZW :], in_=h_late[0][:].rearrange("p c w -> p (c w)"))
 
         out_rows = out_0.rearrange("(p t) c -> p t c", t=PACK)
         size = [keep.tile([P, W], F32, name="size%d" % t) for t in range(PACK)]
-        old = [keep.tile([P, W], F32, name="old%d" % t) for t in range(2)] + size[:2]
+        old = [keep.tile([P, W], F32, name="old%d" % t) for t in range(3)] + size[:1]
         ra = [keep.tile([P, W], F32, name="ra%d" % t) for t in range(PACK)]
         root = [keep.tile([P, W], F32, name="root%d" % u) for u in range(2)]
         work = [keep.tile([P, W], F32, align_bytes=64, name="work%d" % u, tag="work%d" % u) for u in range(2)]
@@ -224,36 +227,42 @@ def tile_picked_tokminmxknorm_none_po_kernel(
         last_columns(1)
         fetch_old(0)
         fetch_pa(0)
-        take_size(0)
-        fetch_old(1)
-        take_root(0)
         last_columns(2)
+        take_size(0)
         last_columns(3)
-        fetch_pa(1)
+        fetch_old(1)
         fetch_old(2)
+        take_root(0)
+        fetch_old(3)
+        fetch_pa(1)
         for t in range(PACK):
             first_factor(t)
             if t + 1 < PACK:
                 take_size(t + 1)
                 take_root(t + 1)
-            if t == 0:
-                fetch_old(3)
             second_factor(t)
             put_back(t)
             if t + 2 < PACK:
                 fetch_pa(t + 2)
         out_woven = keep.tile([P, H, PACK], BF16, align_bytes=64, tag="work1")
-        for t in range(PACK):
+        for t in range(PACK - 1):
             nc.vector.tensor_copy(out=out_woven[:, :, t], in_=h[t][:])
+        halves = (slice(0, H // 2), slice(H // 2, H))
+        for cols in halves:
+            nc.vector.tensor_copy(out=out_woven[:, cols, PACK - 1], in_=h[PACK - 1][:, cols])
 
         out_codes = keep.tile([P, H], U32, align_bytes=64)
         out_scales = keep.tile([P, H], U8, align_bytes=64)
-        nc.vector.quantize_mx(
-            out=out_codes[:].bitcast(FP8X4), scales=out_scales[:], in_=out_woven[:].rearrange("p c t -> p (c t)")
-        )
-        nc.sync.dma_start(out=out_1[0].rearrange("p c t -> p (c t)").bitcast(I32), in_=out_codes[:].bitcast(I32))
+        out_words = out_1[0].rearrange("p c t -> p (c t)").bitcast(I32)
+        for cols in halves:
+            nc.vector.quantize_mx(
+                out=out_codes[:, cols].bitcast(FP8X4),
+                scales=out_scales[:, cols],
+                in_=out_woven[:, cols, :].rearrange("p c t -> p (c t)"),
+            )
+            nc.sync.dma_start(out=out_words[:, cols], in_=out_codes[:, cols].bitcast(I32))
         for q in range(4):
-            queue = nc.scalar if q % 2 == 0 else nc.sync
+            queue = nc.sync if q == 3 else nc.scalar
             queue.dma_start(
                 out=out_2[0][4 * q : 4 * q + 4, :].bitcast(I32), in_=out_scales[32 * q : 32 * q + 4, :].bitcast(I32)
             )

@@ -29,11 +29,11 @@ def load_scale_rows(queue, plane, rows):
 
 
 def by_pairs(rows):
-    return rows.rearrange("p t (c i) -> p c t i", i=4)
+    return rows.rearrange("p t (c i) -> p c t i", i=2)
 
 
 def woven_by_pairs(woven):
-    return woven.rearrange("p (c i) t -> p c t i", i=4)
+    return woven.rearrange("p (c i) t -> p c t i", i=2)
 
 
 def tile_picked_tokminmxknorm_none_po_kernel(
@@ -48,20 +48,17 @@ def tile_picked_tokminmxknorm_none_po_kernel(
         nc.vector.memset(xs_table[:].bitcast(I32), 0)
         offs_sb = keep.tile([P, S // 16], U16)
         nc.sync.dma_start(offs_sb[:], offs)
-        gate = keep.tile([P, PACK], F32)
-        nc.scalar.dma_start(out=gate[:], in_=gt.rearrange("(p t) o -> p (t o)", t=PACK))
-        load_scale_rows(nc.sync, xs_table, x_scales[0])
-        w1_raw = keep.tile([P, 2 * N], U8)
-        nc.sync.dma_start(out=w1_raw[:].bitcast(I32), in_=w1_words[0].bitcast(I32))
         x_table = keep.tile([P, T], I32)
-        nc.sync.dma_start(out=x_table[:], in_=x_words[0].rearrange("p n t -> p (n t)").bitcast(I32))
+        nc.scalar.dma_start(out=x_table[:], in_=x_words[0].rearrange("p n t -> p (n t)").bitcast(I32))
+        load_scale_rows(nc.sync, xs_table, x_scales[0])
         wa_rows = wa.rearrange("(p j) c -> p j c", j=PACK)
         wa_raw = []
         for lo, hi in WA_CHUNKS:
             raw = keep.tile([P, PACK, hi - lo], F32, name="wa_raw%d" % lo)
-            nc.sync.dma_start(out=raw[:], in_=wa_rows[:, :, lo:hi])
+            nc.scalar.dma_start(out=raw[:], in_=wa_rows[:, :, lo:hi])
             wa_raw.append(raw)
-
+        gate = keep.tile([P, PACK], F32)
+        nc.sync.dma_start(out=gate[:], in_=gt.rearrange("(p t) o -> p (t o)", t=PACK))
         n1_sb = keep.tile([P, H // 16], U16)
         nc.sync.dma_start(n1_sb[:], n1)
         n2_sb = keep.tile([P, H // 16], U16)
@@ -69,19 +66,19 @@ def tile_picked_tokminmxknorm_none_po_kernel(
         w1s_raw = keep.tile([P, N], U8)
         nc.gpsimd.memset(w1s_raw[:].bitcast(I32), 0)
         load_scale_rows(nc.sync, w1s_raw, w1_scales[0])
+        w1_raw = keep.tile([P, 2 * N], U8)
+        nc.sync.dma_start(out=w1_raw[:].bitcast(I32), in_=w1_words[0].bitcast(I32))
         n3_sb = keep.tile([P, W // 16], U16)
         nc.sync.dma_start(n3_sb[:], n3)
         n4_sb = keep.tile([P, W // 16], U16)
         nc.sync.dma_start(n4_sb[:], n4)
 
-        w1_dealt = keep.tile([P, PACK, P, 2], U8, align_bytes=64)
-        nc.vector.tensor_copy(out=w1_dealt[:], in_=w1_raw[:].rearrange("p (m t b) -> p t m b", t=PACK, b=2))
+        x_dealt = keep.tile([P, PACK, P], U32, align_bytes=64)
+        nc.vector.tensor_copy(x_dealt[:].rearrange("p t m -> p m t"), x_table[:].bitcast(U32).indirect(offs_sb[:]))
         xs_picked = keep.tile([P, S], U8)
         nc.vector.tensor_copy(xs_picked[:], xs_table[:].indirect(offs_sb[:]))
         xs_dealt = keep.tile([P, PACK, P], U8, align_bytes=64)
         nc.vector.tensor_copy(out=xs_dealt[:], in_=xs_picked[:].rearrange("p (m t) -> p t m", t=PACK))
-        x_dealt = keep.tile([P, PACK, P], U32, align_bytes=64)
-        nc.vector.tensor_copy(x_dealt[:].rearrange("p t m -> p m t"), x_table[:].bitcast(U32).indirect(offs_sb[:]))
 
         warm = keep.tile([P, 1], F32)
         nc.scalar.activation(warm[:], gate[:, 0:1], ACT.Abs_reciprocal_sqrt, bias=0.5)
@@ -95,9 +92,7 @@ def tile_picked_tokminmxknorm_none_po_kernel(
         for half, ((lo, hi), raw) in enumerate(zip(WA_CHUNKS, wa_raw)):
             width = hi - lo
             woven = keep.tile([P, width, PACK], BF16, align_bytes=64, name="wa_woven%d" % lo, tag="wa_woven%d" % lo)
-            split = 96
-            nc.scalar.copy(out=woven_by_pairs(woven[:, :split, :]), in_=by_pairs(raw[:, :, :split]))
-            nc.vector.tensor_copy(out=woven_by_pairs(woven[:, split:, :]), in_=by_pairs(raw[:, :, split:]))
+            nc.scalar.copy(out=woven_by_pairs(woven[:]), in_=by_pairs(raw[:]))
             codes = keep.tile([P, width], U32, align_bytes=64, name="wa_codes%d" % lo)
             scales = keep.tile([P, width], U8, align_bytes=64, name="wa_scales%d" % lo)
             nc.vector.quantize_mx(
@@ -115,13 +110,16 @@ def tile_picked_tokminmxknorm_none_po_kernel(
                     stop=True,
                 )
                 y_banks.append((half, t, lo, hi, bank))
+        w1_both = keep.tile([P, 3 * N], U8, align_bytes=64, tag="wa_woven%d" % WA_CHUNKS[-1][0])
+        w1_dealt = w1_both[:, : 2 * N].rearrange("p (t m b) -> p t m b", t=PACK, b=2)
+        w1s_dealt = w1_both[:, 2 * N :].rearrange("p (t m) -> p t m", t=PACK)
+        nc.vector.tensor_copy(out=w1_dealt, in_=w1_raw[:].rearrange("p (m t b) -> p t m b", t=PACK, b=2))
+        nc.vector.tensor_copy(out=w1s_dealt, in_=w1s_raw[:].rearrange("p (m t) -> p t m", t=PACK))
         for half, t, lo, hi, bank in y_banks:
             if half == 0 or t % 2 == 0:
                 nc.scalar.activation(y[:, t, lo:hi], bank[:], ACT.Copy, scale=gate_abs[:, t : t + 1])
             else:
                 nc.vector.tensor_scalar(y[:, t, lo:hi], bank[:], gate_abs[:, t : t + 1], None, ALU.mult)
-        w1s_dealt = keep.tile([P, PACK, P], U8, align_bytes=64, tag="wa_woven%d" % WA_CHUNKS[-1][0])
-        nc.vector.tensor_copy(out=w1s_dealt[:], in_=w1s_raw[:].rearrange("p (m t) -> p t m", t=PACK))
 
         h = [keep.tile([P, H], F32, name="h%d" % t) for t in range(PACK)]
         h_early = [psum.tile([P, 2, ZW], F32, name="h_early%d" % t, tag="bank%d" % t) for t in range(PACK)]

from contextlib import ExitStack

import concourse.mybir as mybir

K, T, S, N, H, W = 512, 2048, 512, 512, 512, 384
FLOPS = 2 * K * S * H + 2 * S * N * H

F32 = mybir.dt.float32
BF16 = mybir.dt.bfloat16
I32 = mybir.dt.int32
U32 = mybir.dt.uint32
U16 = mybir.dt.uint16
U8 = mybir.dt.uint8
FP8X4 = mybir.dt.float8_e4m3fn_x4
FP4X4 = mybir.dt.float4_e2m1fn_x4
ALU = mybir.AluOpType
ACT = mybir.ActivationFunctionType

P = 128
PACK = 4
WA_CHUNKS = ((0, 256), (256, 512))
ZW = 128
Z_CHUNKS = H // ZW


def load_scale_rows(queue, plane, rows):
    for q in range(4):
        queue.dma_start(out=plane[32 * q : 32 * q + 4, :].bitcast(I32), in_=rows[4 * q : 4 * q + 4, :].bitcast(I32))


def by_pairs(rows):
    return rows.rearrange("p t (c i) -> p c t i", i=2)


def woven_by_pairs(woven):
    return woven.rearrange("p (c i) t -> p c t i", i=2)


def tile_picked_tokminmxknorm_none_po_kernel(
    tc, x_words, x_scales, wa, gt, w1_words, w1_scales, offs, n1, n2, n3, n4, out_0, out_1, out_2
):
    nc = tc.nc
    with ExitStack() as ctx:
        keep = ctx.enter_context(tc.tile_pool(name="keep", bufs=1))
        psum = ctx.enter_context(tc.psum_pool(name="psum", bufs=1))

        xs_table = keep.tile([P, T], U8)
        nc.vector.memset(xs_table[:].bitcast(I32), 0)
        offs_sb = keep.tile([P, S // 16], U16)
        nc.sync.dma_start(offs_sb[:], offs)
        x_table = keep.tile([P, T], I32)
        nc.scalar.dma_start(out=x_table[:], in_=x_words[0].rearrange("p n t -> p (n t)").bitcast(I32))
        load_scale_rows(nc.sync, xs_table, x_scales[0])
        wa_rows = wa.rearrange("(p j) c -> p j c", j=PACK)
        wa_raw = []
        for lo, hi in WA_CHUNKS:
            raw = keep.tile([P, PACK, hi - lo], F32, name="wa_raw%d" % lo)
            nc.scalar.dma_start(out=raw[:], in_=wa_rows[:, :, lo:hi])
            wa_raw.append(raw)
        gate = keep.tile([P, PACK], F32)
        nc.sync.dma_start(out=gate[:], in_=gt.rearrange("(p t) o -> p (t o)", t=PACK))
        n1_sb = keep.tile([P, H // 16], U16)
        nc.sync.dma_start(n1_sb[:], n1)
        n2_sb = keep.tile([P, H // 16], U16)
        nc.sync.dma_start(n2_sb[:], n2)
        w1s_raw = keep.tile([P, N], U8)
        nc.gpsimd.memset(w1s_raw[:].bitcast(I32), 0)
        load_scale_rows(nc.sync, w1s_raw, w1_scales[0])
        w1_raw = keep.tile([P, 2 * N], U8)
        nc.sync.dma_start(out=w1_raw[:].bitcast(I32), in_=w1_words[0].bitcast(I32))
        n3_sb = keep.tile([P, W // 16], U16)
        nc.sync.dma_start(n3_sb[:], n3)
        n4_sb = keep.tile([P, W // 16], U16)
        nc.sync.dma_start(n4_sb[:], n4)

        x_dealt = keep.tile([P, PACK, P], U32, align_bytes=64)
        nc.vector.tensor_copy(x_dealt[:].rearrange("p t m -> p m t"), x_table[:].bitcast(U32).indirect(offs_sb[:]))
        xs_picked = keep.tile([P, S], U8)
        nc.vector.tensor_copy(xs_picked[:], xs_table[:].indirect(offs_sb[:]))
        xs_dealt = keep.tile([P, PACK, P], U8, align_bytes=64)
        nc.vector.tensor_copy(out=xs_dealt[:], in_=xs_picked[:].rearrange("p (m t) -> p t m", t=PACK))

        warm = keep.tile([P, 1], F32)
        nc.scalar.activation(warm[:], gate[:, 0:1], ACT.Abs_reciprocal_sqrt, bias=0.5)
        gate_abs = keep.tile([P, PACK], F32)
        nc.scalar.activation(gate_abs[:], gate[:], ACT.Abs)
        signs = keep.tile([P, PACK], BF16)
        nc.scalar.activation(signs[:], gate[:], ACT.Sign)

        y = keep.tile([P, PACK, H], F32)
        y_banks = []
        for half, ((lo, hi), raw) in enumerate(zip(WA_CHUNKS, wa_raw)):
            width = hi - lo
            woven = keep.tile([P, width, PACK], BF16, align_bytes=64, name="wa_woven%d" % lo, tag="wa_woven%d" % lo)
            nc.scalar.copy(out=woven_by_pairs(woven[:]), in_=by_pairs(raw[:]))
            codes = keep.tile([P, width], U32, align_bytes=64, name="wa_codes%d" % lo)
            scales = keep.tile([P, width], U8, align_bytes=64, name="wa_scales%d" % lo)
            nc.vector.quantize_mx(
                out=codes[:].bitcast(FP8X4), scales=scales[:], in_=woven[:].rearrange("p c t -> p (c t)")
            )
            for t in range(PACK):
                bank = psum.tile([P, width], F32, name="y_bank%d_%d" % (half, t), tag="bank%d" % (PACK * half + t))
                nc.tensor.matmul_mx(
                    out=bank[:],
                    lhsT=x_dealt[:, t, :].bitcast(FP8X4),
                    lhsT_scale=xs_dealt[:, t, :],
                    rhs=codes[:].bitcast(FP8X4),
                    rhs_scale=scales[:],
                    start=True,
                    stop=True,
                )
                y_banks.append((half, t, lo, hi, bank))
        w1_both = keep.tile([P, 3 * N], U8, align_bytes=64, tag="wa_woven%d" % WA_CHUNKS[-1][0])
        w1_dealt = w1_both[:, : 2 * N].rearrange("p (t m b) -> p t m b", t=PACK, b=2)
        w1s_dealt = w1_both[:, 2 * N :].rearrange("p (t m) -> p t m", t=PACK)
        nc.vector.tensor_copy(out=w1_dealt, in_=w1_raw[:].rearrange("p (m t b) -> p t m b", t=PACK, b=2))
        nc.vector.tensor_copy(out=w1s_dealt, in_=w1s_raw[:].rearrange("p (m t) -> p t m", t=PACK))
        for half, t, lo, hi, bank in y_banks:
            if half == 0 or t % 2 == 0:
                nc.scalar.activation(y[:, t, lo:hi], bank[:], ACT.Copy, scale=gate_abs[:, t : t + 1])
            else:
                nc.vector.tensor_scalar(y[:, t, lo:hi], bank[:], gate_abs[:, t : t + 1], None, ALU.mult)

        h = [keep.tile([P, H], F32, name="h%d" % t) for t in range(PACK)]
        h_early = [psum.tile([P, 2, ZW], F32, name="h_early%d" % t, tag="bank%d" % t) for t in range(PACK)]
        h_late = [psum.tile([P, 2, ZW], F32, name="h_late%d" % t, tag="bank%d" % (PACK + t)) for t in range(PACK)]
        y1 = [keep.tile([P, PACK, ZW], F32, name="y1_%d" % c) for c in range(Z_CHUNKS)]
        y2_early = keep.tile([P, PACK, 2 * ZW], F32)
        y2 = [y2_early[:, :, :ZW], y2_early[:, :, ZW:]]
        y2.extend(keep.tile([P, PACK, ZW], F32, name="y2_%d" % c)[:] for c in range(2, Z_CHUNKS))
        larger = [keep.tile([P, PACK, ZW], F32, name="larger%d" % c) for c in range(Z_CHUNKS)]
        z_abs = [keep.tile([P, ZW, PACK], BF16, align_bytes=64, name="z_abs%d" % c) for c in range(Z_CHUNKS)]
        z = [keep.tile([P, ZW, PACK], BF16, align_bytes=64, name="z%d" % c) for c in range(Z_CHUNKS)]

        def fetch(on_scalar, dst, offsets, c, rows):
            for t in rows:
                window = y[:, t, :].indirect(offsets[:, c * ZW // 16 : (c + 1) * ZW // 16])
                if on_scalar:
                    nc.scalar.activation(dst[c][:, t, :], window, ACT.Copy)
                else:
                    nc.vector.tensor_copy(dst[c][:, t, :], window)

        def take_max(c):
            nc.vector.tensor_tensor(larger[c][:], y[:, :, c * ZW : (c + 1) * ZW], y1[c][:], ALU.max)

        def take_min(c):
            nc.vector.tensor_tensor(woven_by_pairs(z_abs[c][:]), by_pairs(larger[c][:]), by_pairs(y2[c]), ALU.min)

        def give_sign(c):
            nc.vector.tensor_tensor(z[c][:], z_abs[c][:], signs[:].unsqueeze(1).to_broadcast([P, ZW, PACK]), ALU.mult)

        def multiply(c):
            codes = keep.tile([P, ZW], U32, align_bytes=64, name="z_codes%d" % c)
            scales = keep.tile([P, ZW], U8, align_bytes=64, name="z_scales%d" % c)
            nc.vector.quantize_mx(
                out=codes[:].bitcast(FP8X4), scales=scales[:], in_=z[c][:].rearrange("p c t -> p (c t)")
            )
            for t in range(PACK):
                nc.tensor.matmul_mx(
                    out=h_early[t][:, c, :] if c < 2 else h_late[t][:, c - 2, :],
                    lhsT=w1_dealt[:, t, :, :].rearrange("p m b -> p (m b)").bitcast(FP4X4),
                    lhsT_scale=w1s_dealt[:, t, :],
                    rhs=codes[:].bitcast(FP8X4),
                    rhs_scale=scales[:],
                    start=True,
                    stop=True,
                )

        every_row = range(PACK)
        for c in range(3):
            fetch(True, y1, n1_sb, c, every_row)
        fetch(True, y2, n2_sb, 2, range(2, 4))
        fetch(True, y1, n1_sb, 3, every_row)
        fetch(True, y2, n2_sb, 3, every_row)
        for t in every_row:
            nc.vector.tensor_copy(y2_early[:, t, :], y[:, t, :].indirect(n2_sb[:, : 2 * ZW // 16]))
        take_max(0)
        fetch(False, y2, n2_sb, 2, range(0, 1))
        take_min(0)
        fetch(False, y2, n2_sb, 2, range(1, 2))
        take_max(1)
        for c in range(Z_CHUNKS):
            give_sign(c)
            if c + 1 < Z_CHUNKS:
                take_min(c + 1)
            multiply(c)
            if c + 2 < Z_CHUNKS:
                take_max(c + 2)
        for t in range(PACK):
            nc.scalar.copy(out=h[t][:, : 2 * ZW], in_=h_early[t][:].rearrange("p c w -> p (c w)"))
        nc.scalar.copy(out=h[0][:, 2 * ZW :], in_=h_late[0][:].rearrange("p c w -> p (c w)"))

        out_rows = out_0.rearrange("(p t) c -> p t c", t=PACK)
        size = [keep.tile([P, W], F32, name="size%d" % t) for t in range(PACK)]
        old = [keep.tile([P, W], F32, name="old%d" % t) for t in range(3)] + size[:1]
        ra = [keep.tile([P, W], F32, name="ra%d" % t) for t in range(PACK)]
        root = [keep.tile([P, W], F32, name="root%d" % u) for u in range(2)]
        work = [keep.tile([P, W], F32, align_bytes=64, name="work%d" % u, tag="work%d" % u) for u in range(2)]

        def last_columns(t):
            nc.vector.tensor_copy(out=h[t][:, 2 * ZW :], in_=h_late[t][:].rearrange("p c w -> p (c w)"))

        def fetch_old(t):
            nc.scalar.activation(old[t][:], h[t][:].indirect(n3_sb[:]), ACT.Copy)

        def fetch_pa(t):
            nc.vector.tensor_copy(work[t % 2][:], h[t][:].indirect(n4_sb[:]))

        def take_size(t):
            nc.vector.scalar_tensor_tensor(size[t][:], work[t % 2][:], -1.0, work[t % 2][:], ALU.mult, ALU.max)

        def take_root(t):
            nc.scalar.activation(root[t % 2][:], size[t][:], ACT.Abs_reciprocal_sqrt, bias=0.5)

        def first_factor(t):
            nc.vector.tensor_tensor(work[t % 2][:], old[t][:], root[t % 2][:], ALU.mult)

        def second_factor(t):
            nc.vector.tensor_tensor(ra[t][:], work[t % 2][:], root[t % 2][:], ALU.mult)

        def put_back(t):
            nc.scalar.activation(h[t][:].indirect(n3_sb[:]), ra[t][:], ACT.Copy)
            nc.sync.dma_start(out=out_rows[:, t, :], in_=h[t][:])

        last_columns(1)
        fetch_old(0)
        fetch_pa(0)
        last_columns(2)
        take_size(0)
        last_columns(3)
        fetch_old(1)
        fetch_old(2)
        take_root(0)
        fetch_old(3)
        fetch_pa(1)
        for t in range(PACK):
            first_factor(t)
            if t + 1 < PACK:
                take_size(t + 1)
                take_root(t + 1)
            second_factor(t)
            put_back(t)
            if t + 2 < PACK:
                fetch_pa(t + 2)
        out_woven = keep.tile([P, H, PACK], BF16, align_bytes=64, tag="work1")
        for t in range(PACK - 1):
            nc.vector.tensor_copy(out=out_woven[:, :, t], in_=h[t][:])
        halves = (slice(0, H // 2), slice(H // 2, H))
        for cols in halves:
            nc.vector.tensor_copy(out=out_woven[:, cols, PACK - 1], in_=h[PACK - 1][:, cols])

        out_codes = keep.tile([P, H], U32, align_bytes=64)
        out_scales = keep.tile([P, H], U8, align_bytes=64)
        out_words = out_1[0].rearrange("p c t -> p (c t)").bitcast(I32)
        for cols in halves:
            nc.vector.quantize_mx(
                out=out_codes[:, cols].bitcast(FP8X4),
                scales=out_scales[:, cols],
                in_=out_woven[:, cols, :].rearrange("p c t -> p (c t)"),
            )
            nc.sync.dma_start(out=out_words[:, cols], in_=out_codes[:, cols].bitcast(I32))
        for q in range(4):
            queue = nc.sync if q == 3 else nc.scalar
            queue.dma_start(
                out=out_2[0][4 * q : 4 * q + 4, :].bitcast(I32), in_=out_scales[32 * q : 32 * q + 4, :].bitcast(I32)
            )
